import numpy as np, ml_dtypes
CORES = [4,20,36,52,68,84,100,116,132,148,164,180,196,212,228,244]
N = 16
VB, TK = 1, 512
def setup_inputs(rng):
    h = rng.standard_normal((128, TK), dtype=np.float32) / 4; w = rng.standard_normal((N, 128, VB * 128), dtype=np.float32)
    a = 2 * np.pi * rng.random((TK)); s = 400 * rng.random((TK)) ** 1.5; h[0] = s * np.cos(a); h[1] = s * np.sin(a); h[2] = 150 * rng.standard_normal((TK)); w[:, 2, :] = 1 + w[:, 2, :] / 50
    a = (2 * np.pi * rng.random() + np.pi / 2 * (rng.permutation(N).reshape(N, 1, 1) + 0.5) / N - 0.5 + (np.arange(VB).reshape(1, VB, 1) + rng.random((N, VB, 128))) / VB).reshape(N, VB * 128); w[:, 0, :] = np.cos(a); w[:, 1, :] = np.sin(a)
    tgt = rng.integers(0, N * VB * 128, size=TK)
    oh = np.zeros((N * VB * 128, TK), np.float32); oh[tgt, np.arange(TK)] = 1.0
    oh = oh.reshape(N, VB, 128, TK).transpose(0, 2, 1, 3).reshape(N, 128, VB * TK)
    return {"h": np.broadcast_to(h, (N, 128, TK)).astype(ml_dtypes.bfloat16), "w": w.astype(ml_dtypes.bfloat16), "oh": oh.astype(ml_dtypes.bfloat16)}
def reference(h, w, oh):
    H, W, OH = h.astype(np.float64), w.astype(np.float64), oh.astype(np.float64)
    Z = np.concatenate([W[r].T @ H[r] for r in range(N)], axis=0)
    O = np.concatenate([OH[r][:, TK * b:TK * b + TK] for r in range(N) for b in range(VB)], axis=0)
    m = Z.max(axis=0)
    l = m + np.log(np.exp(Z - m).sum(axis=0)) - (O * Z).sum(axis=0)
    return {"l": np.broadcast_to(l.astype(np.float32), (N, 1, TK))}

@@ -1,0 +1,155 @@
+from concourse.bass import DstId, RemoteDMATransfer
+from concourse.mybir import AluOpType, AxisListType, ActivationFunctionType
+
+N = 16
+NB = 4
+F32, BF16 = "float32", "bfloat16"
+
+SCRATCH = {
+    "h_sb": ("sbuf", [128, 512], BF16),
+    "w_sb": ("sbuf", [128, 128], BF16),
+    "oh_sb": ("sbuf", [128, 512], BF16),
+    "ones": ("sbuf", [128, 96], F32),
+    "sel": ("sbuf", [128, 96], F32),
+    "ex": ("sbuf", [128, 512], F32),
+    "prod": ("sbuf", [128, 512], F32),
+    "st": ("sbuf", [128, 32], F32),
+    "stT": ("sbuf", [128, 128], F32),
+    "land": ("dram", [N, 128, 12], F32),
+    "y": ("sbuf", [128, 256], F32),
+    "e": ("sbuf", [128, 64], F32),
+    "p": ("sbuf", [128, 64], F32),
+    "nm": ("sbuf", [128, NB], F32),
+    "ss": ("sbuf", [128, NB], F32),
+    "tt": ("sbuf", [128, NB], F32),
+    "cc": ("sbuf", [128, NB], F32),
+    "ln": ("sbuf", [128, NB], F32),
+    "res": ("sbuf", [128, NB], F32),
+    "zt0": ("psum", [128, 512], F32), "zt1": ("psum", [128, 512], F32),
+    "zt2": ("psum", [128, 512], F32), "zt3": ("psum", [128, 512], F32),
+    "z": ("psum", [128, 512], F32),
+    "tp": ("psum", [128, 512], F32),
+    "za": ("psum", [128, 512], F32), "zb": ("psum", [128, 512], F32),
+}
+SEMAPHORES = ["s_h", "s_w", "s_oh", "s_ones", "s_pad", "s_id", "s_mm", "s_max", "s_exp", "s_z", "s_prod", "s_t", "s_tcp",
+              "s_tr", "s_own", "arr", "sent", "s_y", "s_zz", "s_nm", "s_e", "s_tt", "s_p", "s_ss", "s_cc", "s_ln",
+              "s_res", "s_out"]
+
+
+def rank_program(g, core, T, topo):
+    rank = T.rank_of(core)
+    if rank is None:
+        return
+    S = T.sem
+    pe, dve, act, sp = g.tensor, g.vector, g.scalar, g.sync
+    X = AxisListType.X
+    Exp, Ln = ActivationFunctionType.Exp, ActivationFunctionType.Ln
+    zt = [T["zt%d" % b] for b in range(NB)]
+
+    act.dma_start(T.w_sb[:], T.w[:]).then_inc(S.s_w, 16)
+    sp.dma_start(T.h_sb[:], T.h[:]).then_inc(S.s_h, 16)
+    sp.dma_start(T.oh_sb[:], T.oh[:]).then_inc(S.s_oh, 16)
+
+    dve.memset(T.ones[:], 1.0).then_inc(S.s_ones, 1)
+    dve.memset(T.st[:, 12:32], 0.0).then_inc(S.s_pad, 1)
+    g.wait_ge(S.s_ones, 1)
+    g.affine_select(T.sel[0:96, 0:96], T.ones[0:96, 0:96], [[-2, 3], [-1, 2], [-6, 16]],
+                    AluOpType.is_equal, 0.0, 0, 1).then_inc(S.s_id, 1)
+
+    pe.wait_ge(S.s_w, 16)
+    pe.wait_ge(S.s_h, 16)
+    for b in range(NB):
+        pe.matmul(zt[b][:, 0:128], T.h_sb[:, b::NB], T.w_sb[:], True, True).then_inc(S.s_mm, 1)
+    pe.matmul(T.z[:], T.w_sb[:], T.h_sb[:], True, True).then_inc(S.s_z, 1)
+
+    for b in range(NB):
+        dve.wait_ge(S.s_mm, b + 1)
+        dve.tensor_reduce(T.st[:, b:b + 1], zt[b][:, 0:128], X, AluOpType.max, negate=True).then_inc(S.s_max, 1)
+        act.wait_ge(S.s_max, b + 1)
+        act.activation(T.ex[:, 128 * b:128 * b + 128], zt[b][:, 0:128], Exp, bias=T.st[:, b:b + 1], scale=1.0,
+                       accum_out=T.st[:, 4 + b:5 + b]).then_inc(S.s_exp, 1)
+
+    dve.wait_ge(S.s_z, 1)
+    dve.wait_ge(S.s_oh, 16)
+    pe.wait_ge(S.s_ones, 1)
+    for b in range(NB):
+        dve.tensor_tensor(T.prod[:, 128 * b:128 * b + 128], T.z[:, b::NB], T.oh_sb[:, b::NB],
+                          AluOpType.mult).then_inc(S.s_prod, 1)
+        pe.wait_ge(S.s_prod, b + 1)
+        pe.matmul(T.tp[:, b:b + 1], T.prod[:, 128 * b:128 * b + 128], T.ones[:, 0:1], True, True).then_inc(S.s_t, 1)
+    dve.wait_ge(S.s_t, NB)
+    dve.tensor_copy(T.st[:, 8:12], T.tp[:, 0:NB]).then_inc(S.s_tcp, 1)
+
+    dve.wait_ge(S.s_pad, 1)
+    dve.wait_ge(S.s_max, NB)
+    dve.wait_ge(S.s_tcp, 1)
+    dve.wait_ge(S.s_exp, NB)
+    for a in range(4):
+        dve.transpose(T.stT[0:32, 32 * a:32 * a + 32], T.st[32 * a:32 * a + 32, 0:32]).then_inc(S.s_tr, 1)
+    sp.wait_ge(S.s_tr, 4)
+    sp.dma_start(T.land[rank], T.stT[0:12, :]).then_inc(S.s_own, 16)
+
+    others = [T.cores[(rank + 1 + i) % N] for i in range(N - 1)]
+    common = topo.mask(core, others[0])
+    for d in others:
+        common &= topo.mask(core, d)
+    engines = [1 << i for i in range(16) if common & (1 << i)][::2]
+    transfers = []
+    for i, m in enumerate(engines):
+        ds = others[i::len(engines)]
+        ids = []
+        for d in ds:
+            rid, pid = topo.addr(d, core)
+            ids.append(DstId(rid=rid, pnc=pid))
+        transfers.append(RemoteDMATransfer(dst_ids=ids, dma_engine_mask=m, remote_sem=S.arr,
+                                           srcs=[T.land[rank]], dsts=[T.land[rank] for d in ds], alu_op=0))
+    g.wait_ge(S.s_own, 16)
+    g.remote_dma_fused(transfers, local_sem=S.sent)
+    g.wait_ge(S.sent, len(engines))
+
+    sp.wait_ge(S.s_own, 16)
+    sp.wait_ge(S.arr, N - 1)
+    sp.dma_start(T.y[0:96, :], T.land[:]).then_inc(S.s_y, 16)
+
+    pe.wait_ge(S.s_id, 1)
+    pe.wait_ge(S.s_y, 16)
+    zz = [T.za, T.zb]
+    for hb in range(2):
+        pe.matmul(zz[hb][:, 0:96], T.y[0:96, 128 * hb:128 * hb + 128], T.sel[0:96, 0:96], True, True).then_inc(S.s_zz, 1)
+
+    for hb in range(2):
+        dve.wait_ge(S.s_zz, hb + 1)
+        for bh in range(2):
+            b = 2 * bh + hb
+            dve.tensor_reduce(T.nm[:, b:b + 1], zz[hb][:, 16 * bh:16 * bh + 16], X, AluOpType.min).then_inc(S.s_nm, 1)
+    for hb in range(2):
+        act.wait_ge(S.s_nm, 2 * hb + 2)
+        for bh in range(2):
+            b = 2 * bh + hb
+            o = 32 * hb + 16 * bh
+            act.activation(T.e[:, o:o + 16], zz[hb][:, 16 * bh:16 * bh + 16], Exp, bias=T.nm[:, b:b + 1],
+                           scale=-1.0).then_inc(S.s_e, 1)
+    for hb in range(2):
+        dve.wait_ge(S.s_e, 2 * hb + 2)
+        dve.tensor_tensor(T.p[:, 32 * hb:32 * hb + 32], T.e[:, 32 * hb:32 * hb + 32], zz[hb][:, 32:64],
+                          AluOpType.mult).then_inc(S.s_p, 1)
+        for bh in range(2):
+            b = 2 * bh + hb
+            dve.tensor_reduce(T.tt[:, b:b + 1], zz[hb][:, 64 + 16 * bh:80 + 16 * bh], X, AluOpType.add).then_inc(S.s_tt, 1)
+        dve.wait_ge(S.s_p, hb + 1)
+        for bh in range(2):
+            b = 2 * bh + hb
+            o = 32 * hb + 16 * bh
+            dve.tensor_reduce(T.ss[:, b:b + 1], T.p[:, o:o + 16], X, AluOpType.add).then_inc(S.s_ss, 1)
+    act.wait_ge(S.s_ss, NB)
+    act.activation(T.ln[:], T.ss[:], Ln).then_inc(S.s_ln, 1)
+    dve.wait_ge(S.s_nm, NB)
+    dve.wait_ge(S.s_tt, NB)
+    dve.tensor_tensor(T.cc[:], T.nm[:], T.tt[:], AluOpType.add).then_inc(S.s_cc, 1)
+    dve.wait_ge(S.s_cc, 1)
+    dve.wait_ge(S.s_ln, 1)
+    dve.tensor_tensor(T.res[:], T.ln[:], T.cc[:], AluOpType.subtract).then_inc(S.s_res, 1)
+
+    sp.wait_ge(S.s_res, 1)
+    sp.dma_start(T.l[:], T.res[:]).then_inc(S.s_out, 16)
+    sp.wait_ge(S.s_out, 16)

@@ -9,14 +9,19 @@ SCRATCH = {
     "h_sb": ("sbuf", [128, 512], BF16),
     "w_sb": ("sbuf", [128, 128], BF16),
     "oh_sb": ("sbuf", [128, 512], BF16),
-    "ones": ("sbuf", [128, 96], F32),
-    "sel": ("sbuf", [128, 96], F32),
+    "ones": ("sbuf", [128, 64], F32),
+    "selm": ("sbuf", [128, 32], F32),
+    "sels": ("sbuf", [128, 64], F32),
     "ex": ("sbuf", [128, 512], F32),
     "prod": ("sbuf", [128, 512], F32),
-    "st": ("sbuf", [128, 32], F32),
-    "stT": ("sbuf", [128, 128], F32),
-    "land": ("dram", [N, 128, 12], F32),
-    "y": ("sbuf", [128, 256], F32),
+    "stm": ("sbuf", [128, 32], F32),
+    "sts": ("sbuf", [128, 32], F32),
+    "mT": ("sbuf", [128, 128], F32),
+    "sT": ("sbuf", [128, 128], F32),
+    "landm": ("dram", [N, 128, 4], F32),
+    "lands": ("dram", [N, 128, 8], F32),
+    "ym": ("sbuf", [128, 256], F32),
+    "ys": ("sbuf", [128, 256], F32),
     "e": ("sbuf", [128, 64], F32),
     "p": ("sbuf", [128, 64], F32),
     "nm": ("sbuf", [128, NB], F32),
@@ -29,11 +34,10 @@ SCRATCH = {
     "zt2": ("psum", [128, 512], F32), "zt3": ("psum", [128, 512], F32),
     "z": ("psum", [128, 512], F32),
     "tp": ("psum", [128, 512], F32),
-    "za": ("psum", [128, 512], F32), "zb": ("psum", [128, 512], F32),
 }
 SEMAPHORES = ["s_h", "s_w", "s_oh", "s_ones", "s_pad", "s_id", "s_mm", "s_max", "s_exp", "s_z", "s_prod", "s_t", "s_tcp",
-              "s_tr", "s_own", "arr", "sent", "s_y", "s_zz", "s_nm", "s_e", "s_tt", "s_p", "s_ss", "s_cc", "s_ln",
-              "s_res", "s_out"]
+              "s_trm", "s_trs", "s_ownm", "s_owns", "arrm", "arrs", "sent", "s_ym", "s_ys", "s_zm", "s_zs", "s_nm", "s_e",
+              "s_tt", "s_p", "s_ss", "s_cc", "s_ln", "s_res", "s_out"]
 
 
 def rank_program(g, core, T, topo):
@@ -51,9 +55,12 @@ def rank_program(g, core, T, topo):
     sp.dma_start(T.oh_sb[:], T.oh[:]).then_inc(S.s_oh, 16)
 
     dve.memset(T.ones[:], 1.0).then_inc(S.s_ones, 1)
-    dve.memset(T.st[:, 12:32], 0.0).then_inc(S.s_pad, 1)
+    dve.memset(T.stm[:, 4:32], 0.0).then_inc(S.s_pad, 1)
+    dve.memset(T.sts[:, 8:32], 0.0).then_inc(S.s_pad, 1)
     g.wait_ge(S.s_ones, 1)
-    g.affine_select(T.sel[0:96, 0:96], T.ones[0:96, 0:96], [[-2, 3], [-1, 2], [-6, 16]],
+    g.affine_select(T.selm[0:32, 0:32], T.ones[0:32, 0:32], [[-1, 2], [-2, 16]],
+                    AluOpType.is_equal, 0.0, 0, 1).then_inc(S.s_id, 1)
+    g.affine_select(T.sels[0:64, 0:64], T.ones[0:64, 0:64], [[-2, 2], [-1, 2], [-4, 16]],
                     AluOpType.is_equal, 0.0, 0, 1).then_inc(S.s_id, 1)
 
     pe.wait_ge(S.s_w, 16)
@@ -64,10 +71,17 @@ def rank_program(g, core, T, topo):
 
     for b in range(NB):
         dve.wait_ge(S.s_mm, b + 1)
-        dve.tensor_reduce(T.st[:, b:b + 1], zt[b][:, 0:128], X, AluOpType.max, negate=True).then_inc(S.s_max, 1)
+        dve.tensor_reduce(T.stm[:, b:b + 1], zt[b][:, 0:128], X, AluOpType.max, negate=True).then_inc(S.s_max, 1)
         act.wait_ge(S.s_max, b + 1)
-        act.activation(T.ex[:, 128 * b:128 * b + 128], zt[b][:, 0:128], Exp, bias=T.st[:, b:b + 1], scale=1.0,
-                       accum_out=T.st[:, 4 + b:5 + b]).then_inc(S.s_exp, 1)
+        act.activation(T.ex[:, 128 * b:128 * b + 128], zt[b][:, 0:128], Exp, bias=T.stm[:, b:b + 1], scale=1.0,
+                       accum_out=T.sts[:, b:b + 1]).then_inc(S.s_exp, 1)
+
+    dve.wait_ge(S.s_pad, 2)
+    dve.wait_ge(S.s_max, NB)
+    for a in range(4):
+        dve.transpose(T.mT[0:32, 32 * a:32 * a + 32], T.stm[32 * a:32 * a + 32, 0:32]).then_inc(S.s_trm, 1)
+    sp.wait_ge(S.s_trm, 4)
+    sp.dma_start(T.landm[rank], T.mT[0:4, :]).then_inc(S.s_ownm, 16)
 
     dve.wait_ge(S.s_z, 1)
     dve.wait_ge(S.s_oh, 16)
@@ -78,64 +92,74 @@ def rank_program(g, core, T, topo):
         pe.wait_ge(S.s_prod, b + 1)
         pe.matmul(T.tp[:, b:b + 1], T.prod[:, 128 * b:128 * b + 128], T.ones[:, 0:1], True, True).then_inc(S.s_t, 1)
     dve.wait_ge(S.s_t, NB)
-    dve.tensor_copy(T.st[:, 8:12], T.tp[:, 0:NB]).then_inc(S.s_tcp, 1)
+    dve.tensor_copy(T.sts[:, 4:8], T.tp[:, 0:NB]).then_inc(S.s_tcp, 1)
 
-    dve.wait_ge(S.s_pad, 1)
-    dve.wait_ge(S.s_max, NB)
     dve.wait_ge(S.s_tcp, 1)
     dve.wait_ge(S.s_exp, NB)
     for a in range(4):
-        dve.transpose(T.stT[0:32, 32 * a:32 * a + 32], T.st[32 * a:32 * a + 32, 0:32]).then_inc(S.s_tr, 1)
-    sp.wait_ge(S.s_tr, 4)
-    sp.dma_start(T.land[rank], T.stT[0:12, :]).then_inc(S.s_own, 16)
+        dve.transpose(T.sT[0:32, 32 * a:32 * a + 32], T.sts[32 * a:32 * a + 32, 0:32]).then_inc(S.s_trs, 1)
+    sp.wait_ge(S.s_trs, 4)
+    sp.dma_start(T.lands[rank], T.sT[0:8, :]).then_inc(S.s_owns, 16)
 
     others = [T.cores[(rank + 1 + i) % N] for i in range(N - 1)]
     common = topo.mask(core, others[0])
     for d in others:
         common &= topo.mask(core, d)
     engines = [1 << i for i in range(16) if common & (1 << i)][::2]
-    transfers = []
-    for i, m in enumerate(engines):
-        ds = others[i::len(engines)]
-        ids = []
-        for d in ds:
-            rid, pid = topo.addr(d, core)
-            ids.append(DstId(rid=rid, pnc=pid))
-        transfers.append(RemoteDMATransfer(dst_ids=ids, dma_engine_mask=m, remote_sem=S.arr,
-                                           srcs=[T.land[rank]], dsts=[T.land[rank] for d in ds], alu_op=0))
-    g.wait_ge(S.s_own, 16)
-    g.remote_dma_fused(transfers, local_sem=S.sent)
-    g.wait_ge(S.sent, len(engines))
 
-    sp.wait_ge(S.s_own, 16)
-    sp.wait_ge(S.arr, N - 1)
-    sp.dma_start(T.y[0:96, :], T.land[:]).then_inc(S.s_y, 16)
+    def send(slot, sem):
+        transfers = []
+        for i, m in enumerate(engines):
+            ds = others[i::len(engines)]
+            ids = []
+            for d in ds:
+                rid, pid = topo.addr(d, core)
+                ids.append(DstId(rid=rid, pnc=pid))
+            transfers.append(RemoteDMATransfer(dst_ids=ids, dma_engine_mask=m, remote_sem=sem,
+                                               srcs=[slot], dsts=[slot for d in ds], alu_op=0))
+        g.remote_dma_fused(transfers, local_sem=S.sent)
 
-    pe.wait_ge(S.s_id, 1)
-    pe.wait_ge(S.s_y, 16)
-    zz = [T.za, T.zb]
+    g.wait_ge(S.s_ownm, 16)
+    send(T.landm[rank], S.arrm)
+    g.wait_ge(S.s_owns, 16)
+    send(T.lands[rank], S.arrs)
+    g.wait_ge(S.sent, 2 * len(engines))
+
+    sp.wait_ge(S.s_ownm, 16)
+    sp.wait_ge(S.arrm, N - 1)
+    sp.dma_start(T.ym[0:32, :], T.landm[:]).then_inc(S.s_ym, 16)
+    sp.wait_ge(S.s_owns, 16)
+    sp.wait_ge(S.arrs, N - 1)
+    sp.dma_start(T.ys[0:64, :], T.lands[:]).then_inc(S.s_ys, 16)
+
+    pe.wait_ge(S.s_id, 2)
+    pe.wait_ge(S.s_max, NB)
+    pe.wait_ge(S.s_exp, NB)
+    pe.wait_ge(S.s_ym, 16)
     for hb in range(2):
-        pe.matmul(zz[hb][:, 0:96], T.y[0:96, 128 * hb:128 * hb + 128], T.sel[0:96, 0:96], True, True).then_inc(S.s_zz, 1)
+        pe.matmul(zt[hb][:, 0:32], T.ym[0:32, 128 * hb:128 * hb + 128], T.selm[0:32, 0:32], True, True).then_inc(S.s_zm, 1)
+    pe.wait_ge(S.s_ys, 16)
+    for hb in range(2):
+        pe.matmul(zt[2 + hb][:, 0:64], T.ys[0:64, 128 * hb:128 * hb + 128], T.sels[0:64, 0:64], True, True).then_inc(S.s_zs, 1)
 
     for hb in range(2):
-        dve.wait_ge(S.s_zz, hb + 1)
+        dve.wait_ge(S.s_zm, hb + 1)
         for bh in range(2):
             b = 2 * bh + hb
-            dve.tensor_reduce(T.nm[:, b:b + 1], zz[hb][:, 16 * bh:16 * bh + 16], X, AluOpType.min).then_inc(S.s_nm, 1)
+            dve.tensor_reduce(T.nm[:, b:b + 1], zt[hb][:, 16 * bh:16 * bh + 16], X, AluOpType.min).then_inc(S.s_nm, 1)
     for hb in range(2):
         act.wait_ge(S.s_nm, 2 * hb + 2)
         for bh in range(2):
             b = 2 * bh + hb
             o = 32 * hb + 16 * bh
-            act.activation(T.e[:, o:o + 16], zz[hb][:, 16 * bh:16 * bh + 16], Exp, bias=T.nm[:, b:b + 1],
+            act.activation(T.e[:, o:o + 16], zt[hb][:, 16 * bh:16 * bh + 16], Exp, bias=T.nm[:, b:b + 1],
                            scale=-1.0).then_inc(S.s_e, 1)
+
+    dve.wait_ge(S.s_e, NB)
     for hb in range(2):
-        dve.wait_ge(S.s_e, 2 * hb + 2)
-        dve.tensor_tensor(T.p[:, 32 * hb:32 * hb + 32], T.e[:, 32 * hb:32 * hb + 32], zz[hb][:, 32:64],
+        dve.wait_ge(S.s_zs, hb + 1)
+        dve.tensor_tensor(T.p[:, 32 * hb:32 * hb + 32], T.e[:, 32 * hb:32 * hb + 32], zt[2 + hb][:, 0:32],
                           AluOpType.mult).then_inc(S.s_p, 1)
-        for bh in range(2):
-            b = 2 * bh + hb
-            dve.tensor_reduce(T.tt[:, b:b + 1], zz[hb][:, 64 + 16 * bh:80 + 16 * bh], X, AluOpType.add).then_inc(S.s_tt, 1)
         dve.wait_ge(S.s_p, hb + 1)
         for bh in range(2):
             b = 2 * bh + hb
@@ -143,6 +167,11 @@ def rank_program(g, core, T, topo):
             dve.tensor_reduce(T.ss[:, b:b + 1], T.p[:, o:o + 16], X, AluOpType.add).then_inc(S.s_ss, 1)
     act.wait_ge(S.s_ss, NB)
     act.activation(T.ln[:], T.ss[:], Ln).then_inc(S.s_ln, 1)
+
+    for hb in range(2):
+        for bh in range(2):
+            b = 2 * bh + hb
+            dve.tensor_reduce(T.tt[:, b:b + 1], zt[2 + hb][:, 32 + 16 * bh:48 + 16 * bh], X, AluOpType.add).then_inc(S.s_tt, 1)
     dve.wait_ge(S.s_nm, NB)
     dve.wait_ge(S.s_tt, NB)
     dve.tensor_tensor(T.cc[:], T.nm[:], T.tt[:], AluOpType.add).then_inc(S.s_cc, 1)

@@ -4,26 +4,19 @@ from concourse.mybir import AluOpType, AxisListType, ActivationFunctionType
 N = 16
 NB = 4
 F32, BF16 = "float32", "bfloat16"
+KINDS = ("m", "s", "t")
 
 SCRATCH = {
     "h_sb": ("sbuf", [128, 512], BF16),
     "w_sb": ("sbuf", [128, 128], BF16),
     "oh_sb": ("sbuf", [128, 512], BF16),
     "ones": ("sbuf", [128, 64], F32),
-    "selm": ("sbuf", [128, 32], F32),
-    "sels": ("sbuf", [128, 64], F32),
+    "sel": ("sbuf", [128, 64], F32),
     "ex": ("sbuf", [128, 512], F32),
     "prod": ("sbuf", [128, 512], F32),
-    "stm": ("sbuf", [128, 32], F32),
-    "sts": ("sbuf", [128, 32], F32),
-    "mT": ("sbuf", [128, 128], F32),
-    "sT": ("sbuf", [128, 128], F32),
-    "landm": ("dram", [N, 128, 4], F32),
-    "lands": ("dram", [N, 128, 8], F32),
-    "ym": ("sbuf", [128, 256], F32),
-    "ys": ("sbuf", [128, 256], F32),
     "e": ("sbuf", [128, 64], F32),
     "p": ("sbuf", [128, 64], F32),
+    "pc": ("sbuf", [128, 32], F32),
     "nm": ("sbuf", [128, NB], F32),
     "ss": ("sbuf", [128, NB], F32),
     "tt": ("sbuf", [128, NB], F32),
@@ -35,9 +28,15 @@ SCRATCH = {
     "z": ("psum", [128, 512], F32),
     "tp": ("psum", [128, 512], F32),
 }
+for _k in KINDS:
+    SCRATCH["st" + _k] = ("sbuf", [128, 32], F32)
+    SCRATCH["tr" + _k] = ("sbuf", [128, 128], F32)
+    SCRATCH["land" + _k] = ("dram", [N, 128, NB], F32)
+    SCRATCH["y" + _k] = ("sbuf", [128, 128], F32)
 SEMAPHORES = ["s_h", "s_w", "s_oh", "s_ones", "s_pad", "s_id", "s_mm", "s_max", "s_exp", "s_z", "s_prod", "s_t", "s_tcp",
-              "s_trm", "s_trs", "s_ownm", "s_owns", "arrm", "arrs", "sent", "s_ym", "s_ys", "s_zm", "s_zs", "s_nm", "s_e",
-              "s_tt", "s_p", "s_ss", "s_cc", "s_ln", "s_res", "s_out"]
+              "sent", "s_nm", "s_e", "s_tt", "s_p", "s_ss", "s_cc", "s_ln", "s_res", "s_out"]
+for _k in KINDS:
+    SEMAPHORES += ["s_tr" + _k, "s_own" + _k, "arr" + _k, "s_y" + _k, "s_z" + _k]
 
 
 def rank_program(g, core, T, topo):
@@ -47,7 +46,7 @@ def rank_program(g, core, T, topo):
     S = T.sem
     pe, dve, act, sp = g.tensor, g.vector, g.scalar, g.sync
     X = AxisListType.X
-    Exp, Ln = ActivationFunctionType.Exp, ActivationFunctionType.Ln
+    Exp, Ln, Idn = ActivationFunctionType.Exp, ActivationFunctionType.Ln, ActivationFunctionType.Identity
     zt = [T["zt%d" % b] for b in range(NB)]
 
     act.dma_start(T.w_sb[:], T.w[:]).then_inc(S.s_w, 16)
@@ -55,12 +54,10 @@ def rank_program(g, core, T, topo):
     sp.dma_start(T.oh_sb[:], T.oh[:]).then_inc(S.s_oh, 16)
 
     dve.memset(T.ones[:], 1.0).then_inc(S.s_ones, 1)
-    dve.memset(T.stm[:, 4:32], 0.0).then_inc(S.s_pad, 1)
-    dve.memset(T.sts[:, 8:32], 0.0).then_inc(S.s_pad, 1)
+    for k in KINDS:
+        dve.memset(T["st" + k][:, 4:32], 0.0).then_inc(S.s_pad, 1)
     g.wait_ge(S.s_ones, 1)
-    g.affine_select(T.selm[0:32, 0:32], T.ones[0:32, 0:32], [[-1, 2], [-2, 16]],
-                    AluOpType.is_equal, 0.0, 0, 1).then_inc(S.s_id, 1)
-    g.affine_select(T.sels[0:64, 0:64], T.ones[0:64, 0:64], [[-2, 2], [-1, 2], [-4, 16]],
+    g.affine_select(T.sel[0:64, 0:64], T.ones[0:64, 0:64], [[-1, 4], [-4, 16]],
                     AluOpType.is_equal, 0.0, 0, 1).then_inc(S.s_id, 1)
 
     pe.wait_ge(S.s_w, 16)
@@ -76,12 +73,15 @@ def rank_program(g, core, T, topo):
         act.activation(T.ex[:, 128 * b:128 * b + 128], zt[b][:, 0:128], Exp, bias=T.stm[:, b:b + 1], scale=1.0,
                        accum_out=T.sts[:, b:b + 1]).then_inc(S.s_exp, 1)
 
-    dve.wait_ge(S.s_pad, 2)
+    def turn_and_store(k):
+        for a in range(4):
+            dve.transpose(T["tr" + k][0:32, 32 * a:32 * a + 32], T["st" + k][32 * a:32 * a + 32, 0:32]).then_inc(S["s_tr" + k], 1)
+        sp.wait_ge(S["s_tr" + k], 4)
+        sp.dma_start(T["land" + k][rank], T["tr" + k][0:NB, :]).then_inc(S["s_own" + k], 16)
+
+    dve.wait_ge(S.s_pad, 3)
     dve.wait_ge(S.s_max, NB)
-    for a in range(4):
-        dve.transpose(T.mT[0:32, 32 * a:32 * a + 32], T.stm[32 * a:32 * a + 32, 0:32]).then_inc(S.s_trm, 1)
-    sp.wait_ge(S.s_trm, 4)
-    sp.dma_start(T.landm[rank], T.mT[0:4, :]).then_inc(S.s_ownm, 16)
+    turn_and_store("m")
 
     dve.wait_ge(S.s_z, 1)
     dve.wait_ge(S.s_oh, 16)
@@ -91,23 +91,21 @@ def rank_program(g, core, T, topo):
                           AluOpType.mult).then_inc(S.s_prod, 1)
         pe.wait_ge(S.s_prod, b + 1)
         pe.matmul(T.tp[:, b:b + 1], T.prod[:, 128 * b:128 * b + 128], T.ones[:, 0:1], True, True).then_inc(S.s_t, 1)
-    dve.wait_ge(S.s_t, NB)
-    dve.tensor_copy(T.sts[:, 4:8], T.tp[:, 0:NB]).then_inc(S.s_tcp, 1)
 
-    dve.wait_ge(S.s_tcp, 1)
     dve.wait_ge(S.s_exp, NB)
-    for a in range(4):
-        dve.transpose(T.sT[0:32, 32 * a:32 * a + 32], T.sts[32 * a:32 * a + 32, 0:32]).then_inc(S.s_trs, 1)
-    sp.wait_ge(S.s_trs, 4)
-    sp.dma_start(T.lands[rank], T.sT[0:8, :]).then_inc(S.s_owns, 16)
+    turn_and_store("s")
+    dve.wait_ge(S.s_t, NB)
+    dve.tensor_copy(T.stt[:, 0:NB], T.tp[:, 0:NB]).then_inc(S.s_tcp, 1)
+    dve.wait_ge(S.s_tcp, 1)
+    turn_and_store("t")
 
     others = [T.cores[(rank + 1 + i) % N] for i in range(N - 1)]
     common = topo.mask(core, others[0])
     for d in others:
         common &= topo.mask(core, d)
     engines = [1 << i for i in range(16) if common & (1 << i)][::2]
-
-    def send(slot, sem):
+    for k in KINDS:
+        slot = T["land" + k][rank]
         transfers = []
         for i, m in enumerate(engines):
             ds = others[i::len(engines)]
@@ -115,63 +113,48 @@ def rank_program(g, core, T, topo):
             for d in ds:
                 rid, pid = topo.addr(d, core)
                 ids.append(DstId(rid=rid, pnc=pid))
-            transfers.append(RemoteDMATransfer(dst_ids=ids, dma_engine_mask=m, remote_sem=sem,
+            transfers.append(RemoteDMATransfer(dst_ids=ids, dma_engine_mask=m, remote_sem=S["arr" + k],
                                                srcs=[slot], dsts=[slot for d in ds], alu_op=0))
+        g.wait_ge(S["s_own" + k], 16)
         g.remote_dma_fused(transfers, local_sem=S.sent)
+    g.wait_ge(S.sent, 3 * len(engines))
 
-    g.wait_ge(S.s_ownm, 16)
-    send(T.landm[rank], S.arrm)
-    g.wait_ge(S.s_owns, 16)
-    send(T.lands[rank], S.arrs)
-    g.wait_ge(S.sent, 2 * len(engines))
-
-    sp.wait_ge(S.s_ownm, 16)
-    sp.wait_ge(S.arrm, N - 1)
-    sp.dma_start(T.ym[0:32, :], T.landm[:]).then_inc(S.s_ym, 16)
-    sp.wait_ge(S.s_owns, 16)
-    sp.wait_ge(S.arrs, N - 1)
-    sp.dma_start(T.ys[0:64, :], T.lands[:]).then_inc(S.s_ys, 16)
-
-    pe.wait_ge(S.s_id, 2)
+    pe.wait_ge(S.s_id, 1)
     pe.wait_ge(S.s_max, NB)
     pe.wait_ge(S.s_exp, NB)
-    pe.wait_ge(S.s_ym, 16)
-    for hb in range(2):
-        pe.matmul(zt[hb][:, 0:32], T.ym[0:32, 128 * hb:128 * hb + 128], T.selm[0:32, 0:32], True, True).then_inc(S.s_zm, 1)
-    pe.wait_ge(S.s_ys, 16)
-    for hb in range(2):
-        pe.matmul(zt[2 + hb][:, 0:64], T.ys[0:64, 128 * hb:128 * hb + 128], T.sels[0:64, 0:64], True, True).then_inc(S.s_zs, 1)
+    zz = {}
+    for i, k in enumerate(KINDS):
+        sp.wait_ge(S["s_own" + k], 16)
+        sp.wait_ge(S["arr" + k], N - 1)
+        sp.dma_start(T["y" + k][0:64, :], T["land" + k][:]).then_inc(S["s_y" + k], 16)
+        pe.wait_ge(S["s_y" + k], 16)
+        pe.matmul(zt[i][:, 0:64], T["y" + k][0:64, :], T.sel[0:64, 0:64], True, True).then_inc(S["s_z" + k], 1)
+        zz[k] = zt[i]
 
-    for hb in range(2):
-        dve.wait_ge(S.s_zm, hb + 1)
-        for bh in range(2):
-            b = 2 * bh + hb
-            dve.tensor_reduce(T.nm[:, b:b + 1], zt[hb][:, 16 * bh:16 * bh + 16], X, AluOpType.min).then_inc(S.s_nm, 1)
-    for hb in range(2):
-        act.wait_ge(S.s_nm, 2 * hb + 2)
-        for bh in range(2):
-            b = 2 * bh + hb
-            o = 32 * hb + 16 * bh
-            act.activation(T.e[:, o:o + 16], zt[hb][:, 16 * bh:16 * bh + 16], Exp, bias=T.nm[:, b:b + 1],
-                           scale=-1.0).then_inc(S.s_e, 1)
+    dve.wait_ge(S.s_zm, 1)
+    for b in range(NB):
+        dve.tensor_reduce(T.nm[:, b:b + 1], zz["m"][:, 16 * b:16 * b + 16], X, AluOpType.min).then_inc(S.s_nm, 1)
+    act.wait_ge(S.s_nm, NB)
+    for b in range(NB):
+        act.activation(T.e[:, 16 * b:16 * b + 16], zz["m"][:, 16 * b:16 * b + 16], Exp, bias=T.nm[:, b:b + 1],
+                       scale=-1.0).then_inc(S.s_e, 1)
 
     dve.wait_ge(S.s_e, NB)
-    for hb in range(2):
-        dve.wait_ge(S.s_zs, hb + 1)
-        dve.tensor_tensor(T.p[:, 32 * hb:32 * hb + 32], T.e[:, 32 * hb:32 * hb + 32], zt[2 + hb][:, 0:32],
-                          AluOpType.mult).then_inc(S.s_p, 1)
-        dve.wait_ge(S.s_p, hb + 1)
-        for bh in range(2):
-            b = 2 * bh + hb
-            o = 32 * hb + 16 * bh
-            dve.tensor_reduce(T.ss[:, b:b + 1], T.p[:, o:o + 16], X, AluOpType.add).then_inc(S.s_ss, 1)
+    dve.wait_ge(S.s_zs, 1)
+    dve.tensor_tensor(T.p[:], T.e[:], zz["s"][:, 0:64], AluOpType.mult).then_inc(S.s_p, 1)
+    dve.wait_ge(S.s_p, 1)
+    act.wait_ge(S.s_p, 1)
+    for b in range(2):
+        dve.tensor_reduce(T.ss[:, b:b + 1], T.p[:, 16 * b:16 * b + 16], X, AluOpType.add).then_inc(S.s_ss, 1)
+    for b in range(2, NB):
+        act.activation(T.pc[:, 16 * b - 32:16 * b - 16], T.p[:, 16 * b:16 * b + 16], Idn,
+                       accum_out=T.ss[:, b:b + 1]).then_inc(S.s_ss, 1)
     act.wait_ge(S.s_ss, NB)
     act.activation(T.ln[:], T.ss[:], Ln).then_inc(S.s_ln, 1)
 
-    for hb in range(2):
-        for bh in range(2):
-            b = 2 * bh + hb
-            dve.tensor_reduce(T.tt[:, b:b + 1], zt[2 + hb][:, 32 + 16 * bh:48 + 16 * bh], X, AluOpType.add).then_inc(S.s_tt, 1)
+    dve.wait_ge(S.s_zt, 1)
+    for b in range(NB):
+        dve.tensor_reduce(T.tt[:, b:b + 1], zz["t"][:, 16 * b:16 * b + 16], X, AluOpType.add).then_inc(S.s_tt, 1)
     dve.wait_ge(S.s_nm, NB)
     dve.wait_ge(S.s_tt, NB)
     dve.tensor_tensor(T.cc[:], T.nm[:], T.tt[:], AluOpType.add).then_inc(S.s_cc, 1)

from concourse.bass import DstId, RemoteDMATransfer
from concourse.mybir import AluOpType, AxisListType, ActivationFunctionType

N = 16
NB = 4
F32, BF16 = "float32", "bfloat16"
KINDS = ("m", "s", "t")

SCRATCH = {
    "h_sb": ("sbuf", [128, 512], BF16),
    "w_sb": ("sbuf", [128, 128], BF16),
    "oh_sb": ("sbuf", [128, 512], BF16),
    "ones": ("sbuf", [128, 64], F32),
    "sel": ("sbuf", [128, 64], F32),
    "ex": ("sbuf", [128, 512], F32),
    "prod": ("sbuf", [128, 512], F32),
    "e": ("sbuf", [128, 64], F32),
    "p": ("sbuf", [128, 64], F32),
    "pc": ("sbuf", [128, 32], F32),
    "nm": ("sbuf", [128, NB], F32),
    "ss": ("sbuf", [128, NB], F32),
    "tt": ("sbuf", [128, NB], F32),
    "cc": ("sbuf", [128, NB], F32),
    "ln": ("sbuf", [128, NB], F32),
    "res": ("sbuf", [128, NB], F32),
    "zt0": ("psum", [128, 512], F32), "zt1": ("psum", [128, 512], F32),
    "zt2": ("psum", [128, 512], F32), "zt3": ("psum", [128, 512], F32),
    "z": ("psum", [128, 512], F32),
    "tp": ("psum", [128, 512], F32),
}
for _k in KINDS:
    SCRATCH["st" + _k] = ("sbuf", [128, 32], F32)
    SCRATCH["tr" + _k] = ("sbuf", [128, 128], F32)
    SCRATCH["land" + _k] = ("dram", [N, 128, NB], F32)
    SCRATCH["y" + _k] = ("sbuf", [128, 128], F32)
SEMAPHORES = ["s_h", "s_w", "s_oh", "s_ones", "s_pad", "s_id", "s_mm", "s_max", "s_exp", "s_z", "s_prod", "s_t", "s_tcp",
              "sent", "s_nm", "s_e", "s_tt", "s_p", "s_ss", "s_cc", "s_ln", "s_res", "s_out"]
for _k in KINDS:
    SEMAPHORES += ["s_tr" + _k, "s_own" + _k, "arr" + _k, "s_y" + _k, "s_z" + _k]


def rank_program(g, core, T, topo):
    rank = T.rank_of(core)
    if rank is None:
        return
    S = T.sem
    pe, dve, act, sp = g.tensor, g.vector, g.scalar, g.sync
    X = AxisListType.X
    Exp, Ln, Idn = ActivationFunctionType.Exp, ActivationFunctionType.Ln, ActivationFunctionType.Identity
    zt = [T["zt%d" % b] for b in range(NB)]

    act.dma_start(T.w_sb[:], T.w[:]).then_inc(S.s_w, 16)
    sp.dma_start(T.h_sb[:], T.h[:]).then_inc(S.s_h, 16)
    sp.dma_start(T.oh_sb[:], T.oh[:]).then_inc(S.s_oh, 16)

    dve.memset(T.ones[:], 1.0).then_inc(S.s_ones, 1)
    for k in KINDS:
        dve.memset(T["st" + k][:, 4:32], 0.0).then_inc(S.s_pad, 1)
    g.wait_ge(S.s_ones, 1)
    g.affine_select(T.sel[0:64, 0:64], T.ones[0:64, 0:64], [[-1, 4], [-4, 16]],
                    AluOpType.is_equal, 0.0, 0, 1).then_inc(S.s_id, 1)

    pe.wait_ge(S.s_w, 16)
    pe.wait_ge(S.s_h, 16)
    for b in range(NB):
        pe.matmul(zt[b][:, 0:128], T.h_sb[:, b::NB], T.w_sb[:], True, True).then_inc(S.s_mm, 1)
    pe.matmul(T.z[:], T.w_sb[:], T.h_sb[:], True, True).then_inc(S.s_z, 1)

    for b in range(NB):
        dve.wait_ge(S.s_mm, b + 1)
        dve.tensor_reduce(T.stm[:, b:b + 1], zt[b][:, 0:128], X, AluOpType.max, negate=True).then_inc(S.s_max, 1)
        act.wait_ge(S.s_max, b + 1)
        act.activation(T.ex[:, 128 * b:128 * b + 128], zt[b][:, 0:128], Exp, bias=T.stm[:, b:b + 1], scale=1.0,
                       accum_out=T.sts[:, b:b + 1]).then_inc(S.s_exp, 1)

    def turn_and_store(k):
        for a in range(4):
            dve.transpose(T["tr" + k][0:32, 32 * a:32 * a + 32], T["st" + k][32 * a:32 * a + 32, 0:32]).then_inc(S["s_tr" + k], 1)
        sp.wait_ge(S["s_tr" + k], 4)
        sp.dma_start(T["land" + k][rank], T["tr" + k][0:NB, :]).then_inc(S["s_own" + k], 16)

    dve.wait_ge(S.s_pad, 3)
    dve.wait_ge(S.s_max, NB)
    turn_and_store("m")

    dve.wait_ge(S.s_z, 1)
    dve.wait_ge(S.s_oh, 16)
    pe.wait_ge(S.s_ones, 1)
    for b in range(NB):
        dve.tensor_tensor(T.prod[:, 128 * b:128 * b + 128], T.z[:, b::NB], T.oh_sb[:, b::NB],
                          AluOpType.mult).then_inc(S.s_prod, 1)
        pe.wait_ge(S.s_prod, b + 1)
        pe.matmul(T.tp[:, b:b + 1], T.prod[:, 128 * b:128 * b + 128], T.ones[:, 0:1], True, True).then_inc(S.s_t, 1)

    dve.wait_ge(S.s_exp, NB)
    turn_and_store("s")
    dve.wait_ge(S.s_t, NB)
    dve.tensor_copy(T.stt[:, 0:NB], T.tp[:, 0:NB]).then_inc(S.s_tcp, 1)
    dve.wait_ge(S.s_tcp, 1)
    turn_and_store("t")

    others = [T.cores[(rank + 1 + i) % N] for i in range(N - 1)]
    common = topo.mask(core, others[0])
    for d in others:
        common &= topo.mask(core, d)
    engines = [1 << i for i in range(16) if common & (1 << i)][::2]
    for k in KINDS:
        slot = T["land" + k][rank]
        transfers = []
        for i, m in enumerate(engines):
            ds = others[i::len(engines)]
            ids = []
            for d in ds:
                rid, pid = topo.addr(d, core)
                ids.append(DstId(rid=rid, pnc=pid))
            transfers.append(RemoteDMATransfer(dst_ids=ids, dma_engine_mask=m, remote_sem=S["arr" + k],
                                               srcs=[slot], dsts=[slot for d in ds], alu_op=0))
        g.wait_ge(S["s_own" + k], 16)
        g.remote_dma_fused(transfers, local_sem=S.sent)
    g.wait_ge(S.sent, 3 * len(engines))

    pe.wait_ge(S.s_id, 1)
    pe.wait_ge(S.s_max, NB)
    pe.wait_ge(S.s_exp, NB)
    zz = {}
    for i, k in enumerate(KINDS):
        sp.wait_ge(S["s_own" + k], 16)
        sp.wait_ge(S["arr" + k], N - 1)
        sp.dma_start(T["y" + k][0:64, :], T["land" + k][:]).then_inc(S["s_y" + k], 16)
        pe.wait_ge(S["s_y" + k], 16)
        pe.matmul(zt[i][:, 0:64], T["y" + k][0:64, :], T.sel[0:64, 0:64], True, True).then_inc(S["s_z" + k], 1)
        zz[k] = zt[i]

    dve.wait_ge(S.s_zm, 1)
    for b in range(NB):
        dve.tensor_reduce(T.nm[:, b:b + 1], zz["m"][:, 16 * b:16 * b + 16], X, AluOpType.min).then_inc(S.s_nm, 1)
    act.wait_ge(S.s_nm, NB)
    for b in range(NB):
        act.activation(T.e[:, 16 * b:16 * b + 16], zz["m"][:, 16 * b:16 * b + 16], Exp, bias=T.nm[:, b:b + 1],
                       scale=-1.0).then_inc(S.s_e, 1)

    dve.wait_ge(S.s_e, NB)
    dve.wait_ge(S.s_zs, 1)
    dve.tensor_tensor(T.p[:], T.e[:], zz["s"][:, 0:64], AluOpType.mult).then_inc(S.s_p, 1)
    dve.wait_ge(S.s_p, 1)
    act.wait_ge(S.s_p, 1)
    for b in range(2):
        dve.tensor_reduce(T.ss[:, b:b + 1], T.p[:, 16 * b:16 * b + 16], X, AluOpType.add).then_inc(S.s_ss, 1)
    for b in range(2, NB):
        act.activation(T.pc[:, 16 * b - 32:16 * b - 16], T.p[:, 16 * b:16 * b + 16], Idn,
                       accum_out=T.ss[:, b:b + 1]).then_inc(S.s_ss, 1)
    act.wait_ge(S.s_ss, NB)
    act.activation(T.ln[:], T.ss[:], Ln).then_inc(S.s_ln, 1)

    dve.wait_ge(S.s_zt, 1)
    for b in range(NB):
        dve.tensor_reduce(T.tt[:, b:b + 1], zz["t"][:, 16 * b:16 * b + 16], X, AluOpType.add).then_inc(S.s_tt, 1)
    dve.wait_ge(S.s_nm, NB)
    dve.wait_ge(S.s_tt, NB)
    dve.tensor_tensor(T.cc[:], T.nm[:], T.tt[:], AluOpType.add).then_inc(S.s_cc, 1)
    dve.wait_ge(S.s_cc, 1)
    dve.wait_ge(S.s_ln, 1)
    dve.tensor_tensor(T.res[:], T.ln[:], T.cc[:], AluOpType.subtract).then_inc(S.s_res, 1)

    sp.wait_ge(S.s_res, 1)
    sp.dma_start(T.l[:], T.res[:]).then_inc(S.s_out, 16)
    sp.wait_ge(S.s_out, 16)
